import numpy as np
import ml_dtypes


def mxq(x, axis, fmt="e4m3"):
    dtype, down = {"e4m3": (ml_dtypes.float8_e4m3fn, 7), "e5m2": (ml_dtypes.float8_e5m2, 14)}[fmt]
    v = np.moveaxis(np.asarray(x, np.float32).astype(ml_dtypes.bfloat16).astype(np.float64), axis, -1)
    blocks = v.reshape(v.shape[:-1] + (-1, 32))
    amax = np.abs(blocks).max(-1, keepdims=True)
    byte = np.maximum(np.where(amax > 0, np.frexp(amax)[1] - 1 + 127, 0) - down, 1)
    scale = np.exp2(byte - 127.0)
    codes = (blocks / scale).astype(np.float32).astype(dtype).astype(np.float64)
    return np.moveaxis((codes * scale).reshape(v.shape), -1, axis)


WIDE = False


def mx_kscale(k):
    if not WIDE:
        return np.ones(k)
    levels = np.array([10, -10, 5, -5, 0])
    if k % 512:
        return np.exp2(np.random.permutation(np.resize(levels, k // 32))).repeat(32)
    a = np.empty((k // 512, 16))
    for p in range(k // 512):
        a[p, :8] = np.random.permutation(np.resize(levels, 8))
        for g in range(8):
            far = levels[np.abs(levels - a[p, g]) >= 10]
            a[p, g + 8] = far[np.random.randint(len(far))]
    return np.exp2(a.ravel()).repeat(32)


def f64(x):
    return np.asarray(x).astype(np.float64)


def striped(idx):
    return np.tile(idx.reshape(-1, 16).T, (8, 1)).astype(np.uint16)


def unstriped(offs):
    return offs[:16].T.reshape(-1).astype(np.int64)


def pack_weight(w):
    k, n = w.shape
    w = f64(np.asarray(w, np.float32).astype(ml_dtypes.bfloat16)).reshape(k // 32, 32, n)
    amax = np.abs(w).max(1)
    byte = np.clip(np.where(amax > 0, np.frexp(amax)[1] - 1 + 127 - 7, 1), 1, 254)
    scaled = (w * np.exp2(127.0 - byte)[:, None, :]).reshape(k, n).astype(np.float32)
    words = np.ascontiguousarray(scaled.reshape(k // 512, 128, 4, n).transpose(0, 1, 3, 2)).astype(ml_dtypes.float8_e4m3fn).view(np.uint8)
    return words, np.ascontiguousarray(byte.astype(np.uint8).reshape(k // 512, 16, n))


def unpack_weight(words, scales):
    g, p, n, _ = words.shape
    vals = np.ascontiguousarray(words).view(ml_dtypes.float8_e4m3fn).astype(np.float64) * np.repeat(np.exp2(scales.astype(np.float64) - 127.0), 8, axis=1)[..., None]
    return vals.transpose(0, 1, 3, 2).reshape(g * 512, n)


K, T, E, C, N = 2048, 1536, 6, 128, 256


def by_expert(wq, xq):
    return np.concatenate([wq[e].T @ xq[:, e * C:(e + 1) * C] for e in range(E)], axis=1)


def setup_inputs():
    n = np.random.standard_normal
    s = mx_kscale(K)[:, None]
    packed = [pack_weight(m) for m in n((E, K, N)) / np.sqrt(K) / s[None]]
    return {
        "xT": (n((K, T)) * s).astype(np.float32),
        "w_words": np.stack([m[0] for m in packed]),
        "w_scales": np.stack([m[1] for m in packed]),
        "gate": np.tile(np.random.uniform(0.2, 1.0, E * C), (N, 1)).astype(np.float32),
        "offs": striped(np.random.permutation(T)[:E * C]),
    }


def reference(xT, w_words, w_scales, gate, offs):
    idx = unstriped(offs)
    xq = mxq(f64(xT)[:, idx], 0, "e4m3")
    w = np.stack([unpack_weight(w_words[e], w_scales[e]) for e in range(E)])
    y = by_expert(w, xq)
    out = np.zeros((N, T))
    out[:, idx] = f64(gate) * y
    return out

@@ -1,0 +1,102 @@
+from contextlib import ExitStack
+
+import concourse.mybir as mybir
+
+K, T, E, C, N = 2048, 1536, 6, 128, 256
+SLOTS = E * C
+FLOPS = 2 * SLOTS * K * N
+
+F32 = mybir.dt.float32
+BF16 = mybir.dt.bfloat16
+I32 = mybir.dt.int32
+U32 = mybir.dt.uint32
+U16 = mybir.dt.uint16
+U8 = mybir.dt.uint8
+FP8X4 = mybir.dt.float8_e4m3fn_x4
+MULT = mybir.AluOpType.mult
+
+P = 128
+PACK = 4
+PASSES = K // (P * PACK)
+HALVES = N // P
+PAIR = 2
+GROUP = PAIR * C
+GROUPS = SLOTS // GROUP
+
+BODY = ((0, 512, "s"), (512, 512, "v"), (1024, 512, "s"))
+LAST = ((0, 512, "s"), (512, 512, "v"), (1024, 256, "s"), (1280, 256, "v"))
+
+
+def tile_routed_moe_kernel(tc, xT, w_words, w_scales, gate, offs, out):
+    nc = tc.nc
+    x_rows = xT.rearrange("(a p t) n -> a p t n", p=P, t=PACK)
+
+    with ExitStack() as ctx:
+        keep = ctx.enter_context(tc.tile_pool(name="keep", bufs=1))
+        raws = ctx.enter_context(tc.tile_pool(name="raws", bufs=12))
+        stage = ctx.enter_context(tc.tile_pool(name="stage", bufs=6))
+        psum = ctx.enter_context(tc.psum_pool(name="psum", bufs=1))
+
+        offs_t = keep.tile([P, SLOTS // 16], U16, name="offs_t")
+        gate_t = keep.tile([P, SLOTS], F32, name="gate_t")
+        w_t = [keep.tile([P, PASSES, N], I32, name=f"w_{e}", align_bytes=64) for e in range(E)]
+        ws_t = keep.tile([P, E * PASSES, N], U8, name="ws_t", align_bytes=64)
+        x_words = [keep.tile([P, T], U32, name=f"x_words_{a}", align_bytes=64) for a in range(PASSES)]
+        x_bytes = keep.tile([P, T], U8, name="x_bytes", align_bytes=64)
+        g_words = [keep.tile([P, SLOTS], U32, name=f"g_words_{a}", align_bytes=64) for a in range(PASSES)]
+        g_bytes = keep.tile([P, SLOTS], U8, name="g_bytes", align_bytes=64)
+        wins = [keep.tile([P, T], F32, name=f"win_{h}") for h in range(HALVES)]
+
+        nc.gpsimd.memset(x_bytes[:], 0)
+        for h in range(HALVES):
+            nc.gpsimd.memset(wins[h][:], 0.0)
+        nc.vector.memset(ws_t[:].rearrange("p b n -> p (b n)").bitcast(I32), 0)
+
+        first = True
+        for a in range(PASSES):
+            for t0, nt, eng in (LAST if a == PASSES - 1 else BODY):
+                raw = raws.tile([P, PACK, nt], F32, name="raw")
+                nc.sync.dma_start(raw[:], x_rows[a, :, :, t0:t0 + nt])
+                if first:
+                    nc.sync.dma_start(offs_t[:], offs)
+                    first = False
+                il = stage.tile([P, nt, PACK], BF16, name="il", align_bytes=64)
+                if eng == "s":
+                    nc.scalar.copy(il[:], raw[:].rearrange("p t n -> p n t"))
+                else:
+                    nc.vector.tensor_copy(il[:], raw[:].rearrange("p t n -> p n t"))
+                nc.vector.quantize_mx(
+                    out=x_words[a][:, t0:t0 + nt].bitcast(FP8X4),
+                    scales=x_bytes[4 * a:P, t0:t0 + nt],
+                    in_=il[:].rearrange("p n t -> p (n t)"),
+                )
+            nc.vector.tensor_copy(g_words[a][:], x_words[a][:].indirect(offs_t[:]))
+        nc.vector.tensor_copy(g_bytes[:], x_bytes[:].indirect(offs_t[:]))
+
+        nc.sync.dma_start(gate_t[:], gate[0:P, :])
+        sc = w_scales.rearrange("e a q n -> q (e a) n")
+        for q in range(4):
+            nc.sync.dma_start(ws_t[32 * q:32 * q + 4, :, :].bitcast(I32), sc[4 * q:4 * q + 4, :, :].bitcast(I32))
+        for e in range(E):
+            nc.sync.dma_start(w_t[e][:], w_words[e].rearrange("a p n r -> p a (n r)").bitcast(I32))
+
+        for c in range(GROUPS):
+            for h in range(HALVES):
+                acc = psum.tile([P, GROUP], F32, name=f"acc_{c}_{h}")
+                for i in range(PAIR):
+                    e = c * PAIR + i
+                    for a in range(PASSES):
+                        nc.tensor.matmul_mx(
+                            out=acc[:, i * C:(i + 1) * C],
+                            lhsT=w_t[e][:, a, h * P:(h + 1) * P].bitcast(FP8X4),
+                            lhsT_scale=ws_t[:, e * PASSES + a, h * P:(h + 1) * P],
+                            rhs=g_words[a][:, e * C:(e + 1) * C].bitcast(FP8X4),
+                            rhs_scale=g_bytes[4 * a:P, e * C:(e + 1) * C],
+                            start=(a == 0),
+                            stop=(a == PASSES - 1),
+                        )
+                y = stage.tile([P, GROUP], F32, name="y")
+                nc.vector.tensor_tensor(y[:], acc[:], gate_t[:, c * GROUP:(c + 1) * GROUP], MULT)
+                nc.vector.tensor_copy(wins[h][:].indirect(offs_t[:, c * (GROUP // 16):(c + 1) * (GROUP // 16)]), y[:])
+        for h in range(HALVES):
+            nc.sync.dma_start(out[h * P:(h + 1) * P, :], wins[h][:])

@@ -22,9 +22,15 @@ HALVES = N // P
 PAIR = 2
 GROUP = PAIR * C
 GROUPS = SLOTS // GROUP
+BANK = 512
 
-BODY = ((0, 512, "s"), (512, 512, "v"), (1024, 512, "s"))
-LAST = ((0, 512, "s"), (512, 512, "v"), (1024, 256, "s"), (1280, 256, "v"))
+LOADS = (
+    ((0, 1536, ((0, 512, (("s", 512),)), (1024, 512, (("v", 512),)), (512, 512, (("s", 256), ("v", 256))))),),
+    ((0, 1536, ((0, 512, (("s", 512),)), (1024, 512, (("v", 512),)), (512, 512, (("s", 256), ("v", 256))))),),
+    ((0, 1024, ((0, 512, (("s", 512),)), (512, 512, (("v", 512),)))), (1024, 512, ((1024, 512, (("s", 256), ("v", 256))),))),
+    ((0, 1024, ((0, 512, (("s", 512),)), (512, 512, (("v", 512),)))), (1024, 512, ((1024, 512, (("s", 192), ("v", 320))),))),
+)
+GATHERS = ((0, 256), (256, 512))
 
 
 def tile_routed_moe_kernel(tc, xT, w_words, w_scales, gate, offs, out):
@@ -33,70 +39,113 @@ def tile_routed_moe_kernel(tc, xT, w_words, w_scales, gate, offs, out):
 
     with ExitStack() as ctx:
         keep = ctx.enter_context(tc.tile_pool(name="keep", bufs=1))
-        raws = ctx.enter_context(tc.tile_pool(name="raws", bufs=12))
         stage = ctx.enter_context(tc.tile_pool(name="stage", bufs=6))
         psum = ctx.enter_context(tc.psum_pool(name="psum", bufs=1))
 
         offs_t = keep.tile([P, SLOTS // 16], U16, name="offs_t")
+        gate_row = keep.tile([P, SLOTS], F32, name="gate_row")
         gate_t = keep.tile([P, SLOTS], F32, name="gate_t")
-        w_t = [keep.tile([P, PASSES, N], I32, name=f"w_{e}", align_bytes=64) for e in range(E)]
-        ws_t = keep.tile([P, E * PASSES, N], U8, name="ws_t", align_bytes=64)
+        ones = keep.tile([P, P], F32, name="ones")
+        w_t = [keep.tile([P, PAIR * PASSES, N], I32, name=f"w_{c}", align_bytes=64) for c in range(GROUPS)]
+        ws_t = [keep.tile([P, PAIR * PASSES, N], U8, name=f"ws_{c}", align_bytes=64) for c in range(GROUPS)]
         x_words = [keep.tile([P, T], U32, name=f"x_words_{a}", align_bytes=64) for a in range(PASSES)]
         x_bytes = keep.tile([P, T], U8, name="x_bytes", align_bytes=64)
         g_words = [keep.tile([P, SLOTS], U32, name=f"g_words_{a}", align_bytes=64) for a in range(PASSES)]
         g_bytes = keep.tile([P, SLOTS], U8, name="g_bytes", align_bytes=64)
         wins = [keep.tile([P, T], F32, name=f"win_{h}") for h in range(HALVES)]
 
+        nc.gpsimd.memset(gate_row[:], 0.0)
+        nc.gpsimd.memset(ones[:], 1.0)
         nc.gpsimd.memset(x_bytes[:], 0)
+        for c in range(GROUPS):
+            nc.vector.memset(ws_t[c][:].rearrange("p b n -> p (b n)").bitcast(I32), 0)
         for h in range(HALVES):
             nc.gpsimd.memset(wins[h][:], 0.0)
-        nc.vector.memset(ws_t[:].rearrange("p b n -> p (b n)").bitcast(I32), 0)
 
-        first = True
+        def gather_words(a, s0, ns):
+            cols = offs_t[:, s0 // 16:(s0 + ns) // 16]
+            nc.vector.tensor_copy(g_words[a][:, s0:s0 + ns], x_words[a][:].indirect(cols))
+
+        def gather_bytes(s0, ns):
+            cols = offs_t[:, s0 // 16:(s0 + ns) // 16]
+            nc.vector.tensor_copy(g_bytes[:, s0:s0 + ns], x_bytes[:].indirect(cols))
+
         for a in range(PASSES):
-            for t0, nt, eng in (LAST if a == PASSES - 1 else BODY):
-                raw = raws.tile([P, PACK, nt], F32, name="raw")
-                nc.sync.dma_start(raw[:], x_rows[a, :, :, t0:t0 + nt])
-                if first:
+            for (l0, ln, pieces) in LOADS[a]:
+                raw = keep.tile([P, PACK, ln], F32, name=f"raw_{a}_{l0}")
+                nc.sync.dma_start(raw[:], x_rows[a, :, :, l0:l0 + ln])
+                if a == 0 and l0 == 0:
                     nc.sync.dma_start(offs_t[:], offs)
-                    first = False
-                il = stage.tile([P, nt, PACK], BF16, name="il", align_bytes=64)
-                if eng == "s":
-                    nc.scalar.copy(il[:], raw[:].rearrange("p t n -> p n t"))
-                else:
-                    nc.vector.tensor_copy(il[:], raw[:].rearrange("p t n -> p n t"))
-                nc.vector.quantize_mx(
-                    out=x_words[a][:, t0:t0 + nt].bitcast(FP8X4),
-                    scales=x_bytes[4 * a:P, t0:t0 + nt],
-                    in_=il[:].rearrange("p n t -> p (n t)"),
-                )
-            nc.vector.tensor_copy(g_words[a][:], x_words[a][:].indirect(offs_t[:]))
-        nc.vector.tensor_copy(g_bytes[:], x_bytes[:].indirect(offs_t[:]))
+                    nc.sync.dma_start(gate_row[0:1, :], gate[0:1, :])
+                for (t0, nt, shares) in pieces:
+                    il = stage.tile([P, nt, PACK], BF16, name="il", align_bytes=64)
+                    c0 = 0
+                    for (eng, cn) in shares:
+                        src = raw[:, :, t0 - l0 + c0:t0 - l0 + c0 + cn].rearrange("p t (c i) -> p c t i", i=4)
+                        dst = il[:, c0:c0 + cn, :].rearrange("p (c i) t -> p c t i", i=4)
+                        if eng == "s":
+                            nc.scalar.copy(dst, src)
+                        else:
+                            nc.vector.tensor_copy(dst, src)
+                        c0 += cn
+                    nc.vector.quantize_mx(
+                        out=x_words[a][:, t0:t0 + nt].bitcast(FP8X4),
+                        scales=x_bytes[4 * a:P, t0:t0 + nt],
+                        in_=il[:].rearrange("p n t -> p (n t)"),
+                    )
+            if a == 0:
+                for s0 in range(0, SLOTS, BANK):
+                    ns = min(BANK, SLOTS - s0)
+                    spread = psum.tile([P, ns], F32, name=f"spread_{s0}")
+                    nc.tensor.matmul(spread[:], ones[:], gate_row[:, s0:s0 + ns], start=True, stop=True)
+                    nc.scalar.copy(gate_t[:, s0:s0 + ns], spread[:])
+            if a < PASSES - 1:
+                gather_words(a, 0, SLOTS)
+        for s0, ns in GATHERS:
+            gather_words(PASSES - 1, s0, ns)
+            gather_bytes(s0, ns)
 
-        nc.sync.dma_start(gate_t[:], gate[0:P, :])
-        sc = w_scales.rearrange("e a q n -> q (e a) n")
-        for q in range(4):
-            nc.sync.dma_start(ws_t[32 * q:32 * q + 4, :, :].bitcast(I32), sc[4 * q:4 * q + 4, :, :].bitcast(I32))
-        for e in range(E):
-            nc.sync.dma_start(w_t[e][:], w_words[e].rearrange("a p n r -> p a (n r)").bitcast(I32))
+        w_rows = w_words.rearrange("(c e) a p n r -> c p (e a) (n r)", e=PAIR)
+        s_rows = w_scales.rearrange("(c e) a q n -> c q (e a) n", e=PAIR)
+
+        def load_scales(c):
+            for i in range(4):
+                nc.sync.dma_start(ws_t[c][i:P:32, :, :].bitcast(I32), s_rows[c, i:16:4, :, :].bitcast(I32))
+
+        load_scales(0)
+        for h in range(HALVES):
+            cols = slice(h * P, (h + 1) * P)
+            nc.sync.dma_start(w_t[0][:, :, cols], w_rows[0].bitcast(I32)[:, :, cols])
+        for c in range(1, GROUPS):
+            load_scales(c)
+        for c in range(1, GROUPS):
+            for i in range(PAIR):
+                b = slice(i * PASSES, (i + 1) * PASSES)
+                nc.sync.dma_start(w_t[c][:, b, :], w_rows[c, :, b, :].bitcast(I32))
 
         for c in range(GROUPS):
             for h in range(HALVES):
+                cols = slice(h * P, (h + 1) * P)
                 acc = psum.tile([P, GROUP], F32, name=f"acc_{c}_{h}")
                 for i in range(PAIR):
-                    e = c * PAIR + i
+                    slots = slice(c * GROUP + i * C, c * GROUP + (i + 1) * C)
                     for a in range(PASSES):
                         nc.tensor.matmul_mx(
                             out=acc[:, i * C:(i + 1) * C],
-                            lhsT=w_t[e][:, a, h * P:(h + 1) * P].bitcast(FP8X4),
-                            lhsT_scale=ws_t[:, e * PASSES + a, h * P:(h + 1) * P],
-                            rhs=g_words[a][:, e * C:(e + 1) * C].bitcast(FP8X4),
-                            rhs_scale=g_bytes[4 * a:P, e * C:(e + 1) * C],
+                            lhsT=w_t[c][:, i * PASSES + a, cols].bitcast(FP8X4),
+                            lhsT_scale=ws_t[c][:, i * PASSES + a, cols],
+                            rhs=g_words[a][:, slots].bitcast(FP8X4),
+                            rhs_scale=g_bytes[4 * a:P, slots],
                             start=(a == 0),
                             stop=(a == PASSES - 1),
                         )
                 y = stage.tile([P, GROUP], F32, name="y")
-                nc.vector.tensor_tensor(y[:], acc[:], gate_t[:, c * GROUP:(c + 1) * GROUP], MULT)
-                nc.vector.tensor_copy(wins[h][:].indirect(offs_t[:, c * (GROUP // 16):(c + 1) * (GROUP // 16)]), y[:])
+                nc.scalar.copy(y[:], acc[:])
+                nc.vector.tensor_tensor(
+                    wins[h][:].indirect(offs_t[:, c * (GROUP // 16):(c + 1) * (GROUP // 16)]),
+                    y[:],
+                    gate_t[:, c * GROUP:(c + 1) * GROUP],
+                    MULT,
+                )
         for h in range(HALVES):
             nc.sync.dma_start(out[h * P:(h + 1) * P, :], wins[h][:])

from contextlib import ExitStack

import concourse.mybir as mybir

K, T, E, C, N = 2048, 1536, 6, 128, 256
SLOTS = E * C
FLOPS = 2 * SLOTS * K * N

F32 = mybir.dt.float32
BF16 = mybir.dt.bfloat16
I32 = mybir.dt.int32
U32 = mybir.dt.uint32
U16 = mybir.dt.uint16
U8 = mybir.dt.uint8
FP8X4 = mybir.dt.float8_e4m3fn_x4
MULT = mybir.AluOpType.mult

P = 128
PACK = 4
PASSES = K // (P * PACK)
HALVES = N // P
PAIR = 2
GROUP = PAIR * C
GROUPS = SLOTS // GROUP
BANK = 512

LOADS = (
    ((0, 1536, ((0, 512, (("s", 512),)), (1024, 512, (("v", 512),)), (512, 512, (("s", 256), ("v", 256))))),),
    ((0, 1536, ((0, 512, (("s", 512),)), (1024, 512, (("v", 512),)), (512, 512, (("s", 256), ("v", 256))))),),
    ((0, 1024, ((0, 512, (("s", 512),)), (512, 512, (("v", 512),)))), (1024, 512, ((1024, 512, (("s", 256), ("v", 256))),))),
    ((0, 1024, ((0, 512, (("s", 512),)), (512, 512, (("v", 512),)))), (1024, 512, ((1024, 512, (("s", 192), ("v", 320))),))),
)
GATHERS = ((0, 256), (256, 512))


def tile_routed_moe_kernel(tc, xT, w_words, w_scales, gate, offs, out):
    nc = tc.nc
    x_rows = xT.rearrange("(a p t) n -> a p t n", p=P, t=PACK)

    with ExitStack() as ctx:
        keep = ctx.enter_context(tc.tile_pool(name="keep", bufs=1))
        stage = ctx.enter_context(tc.tile_pool(name="stage", bufs=6))
        psum = ctx.enter_context(tc.psum_pool(name="psum", bufs=1))

        offs_t = keep.tile([P, SLOTS // 16], U16, name="offs_t")
        gate_row = keep.tile([P, SLOTS], F32, name="gate_row")
        gate_t = keep.tile([P, SLOTS], F32, name="gate_t")
        ones = keep.tile([P, P], F32, name="ones")
        w_t = [keep.tile([P, PAIR * PASSES, N], I32, name=f"w_{c}", align_bytes=64) for c in range(GROUPS)]
        ws_t = [keep.tile([P, PAIR * PASSES, N], U8, name=f"ws_{c}", align_bytes=64) for c in range(GROUPS)]
        x_words = [keep.tile([P, T], U32, name=f"x_words_{a}", align_bytes=64) for a in range(PASSES)]
        x_bytes = keep.tile([P, T], U8, name="x_bytes", align_bytes=64)
        g_words = [keep.tile([P, SLOTS], U32, name=f"g_words_{a}", align_bytes=64) for a in range(PASSES)]
        g_bytes = keep.tile([P, SLOTS], U8, name="g_bytes", align_bytes=64)
        wins = [keep.tile([P, T], F32, name=f"win_{h}") for h in range(HALVES)]

        nc.gpsimd.memset(gate_row[:], 0.0)
        nc.gpsimd.memset(ones[:], 1.0)
        nc.gpsimd.memset(x_bytes[:], 0)
        for c in range(GROUPS):
            nc.vector.memset(ws_t[c][:].rearrange("p b n -> p (b n)").bitcast(I32), 0)
        for h in range(HALVES):
            nc.gpsimd.memset(wins[h][:], 0.0)

        def gather_words(a, s0, ns):
            cols = offs_t[:, s0 // 16:(s0 + ns) // 16]
            nc.vector.tensor_copy(g_words[a][:, s0:s0 + ns], x_words[a][:].indirect(cols))

        def gather_bytes(s0, ns):
            cols = offs_t[:, s0 // 16:(s0 + ns) // 16]
            nc.vector.tensor_copy(g_bytes[:, s0:s0 + ns], x_bytes[:].indirect(cols))

        for a in range(PASSES):
            for (l0, ln, pieces) in LOADS[a]:
                raw = keep.tile([P, PACK, ln], F32, name=f"raw_{a}_{l0}")
                nc.sync.dma_start(raw[:], x_rows[a, :, :, l0:l0 + ln])
                if a == 0 and l0 == 0:
                    nc.sync.dma_start(offs_t[:], offs)
                    nc.sync.dma_start(gate_row[0:1, :], gate[0:1, :])
                for (t0, nt, shares) in pieces:
                    il = stage.tile([P, nt, PACK], BF16, name="il", align_bytes=64)
                    c0 = 0
                    for (eng, cn) in shares:
                        src = raw[:, :, t0 - l0 + c0:t0 - l0 + c0 + cn].rearrange("p t (c i) -> p c t i", i=4)
                        dst = il[:, c0:c0 + cn, :].rearrange("p (c i) t -> p c t i", i=4)
                        if eng == "s":
                            nc.scalar.copy(dst, src)
                        else:
                            nc.vector.tensor_copy(dst, src)
                        c0 += cn
                    nc.vector.quantize_mx(
                        out=x_words[a][:, t0:t0 + nt].bitcast(FP8X4),
                        scales=x_bytes[4 * a:P, t0:t0 + nt],
                        in_=il[:].rearrange("p n t -> p (n t)"),
                    )
            if a == 0:
                for s0 in range(0, SLOTS, BANK):
                    ns = min(BANK, SLOTS - s0)
                    spread = psum.tile([P, ns], F32, name=f"spread_{s0}")
                    nc.tensor.matmul(spread[:], ones[:], gate_row[:, s0:s0 + ns], start=True, stop=True)
                    nc.scalar.copy(gate_t[:, s0:s0 + ns], spread[:])
            if a < PASSES - 1:
                gather_words(a, 0, SLOTS)
        for s0, ns in GATHERS:
            gather_words(PASSES - 1, s0, ns)
            gather_bytes(s0, ns)

        w_rows = w_words.rearrange("(c e) a p n r -> c p (e a) (n r)", e=PAIR)
        s_rows = w_scales.rearrange("(c e) a q n -> c q (e a) n", e=PAIR)

        def load_scales(c):
            for i in range(4):
                nc.sync.dma_start(ws_t[c][i:P:32, :, :].bitcast(I32), s_rows[c, i:16:4, :, :].bitcast(I32))

        load_scales(0)
        for h in range(HALVES):
            cols = slice(h * P, (h + 1) * P)
            nc.sync.dma_start(w_t[0][:, :, cols], w_rows[0].bitcast(I32)[:, :, cols])
        for c in range(1, GROUPS):
            load_scales(c)
        for c in range(1, GROUPS):
            for i in range(PAIR):
                b = slice(i * PASSES, (i + 1) * PASSES)
                nc.sync.dma_start(w_t[c][:, b, :], w_rows[c, :, b, :].bitcast(I32))

        for c in range(GROUPS):
            for h in range(HALVES):
                cols = slice(h * P, (h + 1) * P)
                acc = psum.tile([P, GROUP], F32, name=f"acc_{c}_{h}")
                for i in range(PAIR):
                    slots = slice(c * GROUP + i * C, c * GROUP + (i + 1) * C)
                    for a in range(PASSES):
                        nc.tensor.matmul_mx(
                            out=acc[:, i * C:(i + 1) * C],
                            lhsT=w_t[c][:, i * PASSES + a, cols].bitcast(FP8X4),
                            lhsT_scale=ws_t[c][:, i * PASSES + a, cols],
                            rhs=g_words[a][:, slots].bitcast(FP8X4),
                            rhs_scale=g_bytes[4 * a:P, slots],
                            start=(a == 0),
                            stop=(a == PASSES - 1),
                        )
                y = stage.tile([P, GROUP], F32, name="y")
                nc.scalar.copy(y[:], acc[:])
                nc.vector.tensor_tensor(
                    wins[h][:].indirect(offs_t[:, c * (GROUP // 16):(c + 1) * (GROUP // 16)]),
                    y[:],
                    gate_t[:, c * GROUP:(c + 1) * GROUP],
                    MULT,
                )
        for h in range(HALVES):
            nc.sync.dma_start(out[h * P:(h + 1) * P, :], wins[h][:])
